import numpy as np
import ml_dtypes


def mxq(x, axis, fmt="e4m3"):
    dtype, down = {"e4m3": (ml_dtypes.float8_e4m3fn, 7), "e5m2": (ml_dtypes.float8_e5m2, 14)}[fmt]
    v = np.moveaxis(np.asarray(x, np.float32).astype(ml_dtypes.bfloat16).astype(np.float64), axis, -1)
    blocks = v.reshape(v.shape[:-1] + (-1, 32))
    amax = np.abs(blocks).max(-1, keepdims=True)
    byte = np.maximum(np.where(amax > 0, np.frexp(amax)[1] - 1 + 127, 0) - down, 1)
    scale = np.exp2(byte - 127.0)
    codes = (blocks / scale).astype(np.float32).astype(dtype).astype(np.float64)
    return np.moveaxis((codes * scale).reshape(v.shape), -1, axis)


WIDE = False


def mx_kscale(k):
    if not WIDE:
        return np.ones(k)
    levels = np.array([10, -10, 5, -5, 0])
    if k % 512:
        return np.exp2(np.random.permutation(np.resize(levels, k // 32))).repeat(32)
    a = np.empty((k // 512, 16))
    for p in range(k // 512):
        a[p, :8] = np.random.permutation(np.resize(levels, 8))
        for g in range(8):
            far = levels[np.abs(levels - a[p, g]) >= 10]
            a[p, g + 8] = far[np.random.randint(len(far))]
    return np.exp2(a.ravel()).repeat(32)


def f64(x):
    return np.asarray(x).astype(np.float64)


def striped(idx):
    return np.tile(np.asarray(idx).reshape(-1, 16).T, (8, 1)).astype(np.uint16)


def unstriped(offs):
    return offs[:16].T.reshape(-1).astype(np.int64)


E2M1 = np.array([0.0, 0.5, 1.0, 1.5, 2.0, 3.0, 4.0, 6.0, -0.0, -0.5, -1.0, -1.5, -2.0, -3.0, -4.0, -6.0])


def pack_weight(w, fmt):
    k, n = w.shape
    w = f64(np.asarray(w, np.float32).astype(ml_dtypes.bfloat16)).reshape(k // 32, 32, n)
    amax = np.abs(w).max(1)
    if fmt == "e4m3":
        byte = np.frexp(amax)[1] - 1 + 127 - 7
    else:
        mant, ex = np.frexp(amax / 6.0)
        byte = np.where(mant > 0.5, ex, ex - 1) + 127
    byte = np.clip(np.where(amax > 0, byte, 1), 1, 254)
    scaled = (w * np.exp2(127.0 - byte)[:, None, :]).reshape(k, n).astype(np.float32)
    by_word = np.ascontiguousarray(scaled.reshape(k // 512, 128, 4, n).transpose(0, 1, 3, 2))
    if fmt == "e4m3":
        words = by_word.astype(ml_dtypes.float8_e4m3fn).view(np.uint8)
    else:
        c = by_word.astype(ml_dtypes.float4_e2m1fn).view(np.uint8) & 0xF
        words = (c[..., 0::2] | (c[..., 1::2] << 4)).reshape(k // 512, 128, 2 * n)
    return np.ascontiguousarray(words), np.ascontiguousarray(byte.astype(np.uint8).reshape(k // 512, 16, n))


def unpack_weight(words, scales, fmt):
    g, _, n = scales.shape
    words = np.ascontiguousarray(words).reshape(g, 128, n, -1)
    if fmt == "e4m3":
        vals = words.view(ml_dtypes.float8_e4m3fn).astype(np.float64)
    else:
        nib = np.empty((g, 128, n, 4), np.uint8)
        nib[..., 0::2] = words & 0xF
        nib[..., 1::2] = words >> 4
        vals = E2M1[nib]
    vals = vals * np.repeat(np.exp2(scales.astype(np.float64) - 127.0), 8, axis=1)[..., None]
    return vals.transpose(0, 1, 3, 2).reshape(g * 512, n)


def bf(x):
    return np.asarray(x, np.float32).astype(ml_dtypes.bfloat16)


def planes(Y):
    r, m = Y.shape
    b = f64(bf(Y)).reshape(r // 32, 32, m)
    amax = np.abs(b).max(1)
    byte = np.clip(np.where(amax > 0, np.frexp(amax)[1] - 1 + 127 - 7, 1), 1, 254)
    codes = (b * np.exp2(127.0 - byte)[:, None, :]).reshape(r, m).astype(np.float32).astype(ml_dtypes.float8_e4m3fn).view(np.uint8)
    words = codes.reshape(r // 512, 128, 4, m).transpose(0, 1, 3, 2)
    return np.ascontiguousarray(words), np.ascontiguousarray(byte.astype(np.uint8).reshape(r // 512, 16, m))


D, T, I, J, U, Z, E, M = 512, 2048, 512, 512, 1024, 1024, 512, 1024


def setup_inputs():
    n = np.random.standard_normal
    idx = np.random.permutation(T)[:I]
    idx2 = np.random.permutation(U)[:J]
    idx3 = np.random.permutation(Z)[:J]
    idx4 = np.random.permutation(M)[:J]
    fd = mx_kscale(D)
    fi = mx_kscale(I)
    ti = np.ones(T)
    ti[idx] = fi
    keysp = pack_weight(n((D, T)) / fd[:, None], "e2m1")
    return {
        "keys_words": keysp[0],
        "keys_scales": keysp[1],
        "notes": (n((D, U)) * 1.0 / np.sqrt(D) * fd[:, None]).astype(np.float32),
        "given": (np.random.uniform(0.3, 1.7, (I, Z))).astype(np.float32),
        "rowf": (np.random.uniform(0.02, 0.08, (I, 1)) * fi[:, None]).astype(np.float32),
        "vals": (n((E, T)) / ti).astype(np.float32),
        "old": (1.0 * n((E, M))).astype(np.float32),
        "offs": striped(idx),
        "offs2": striped(idx2),
        "offs3": striped(idx3),
        "offs4": striped(idx4),
    }


def reference(keys_words, keys_scales, notes, given, rowf, vals, old, offs, offs2, offs3, offs4):
    idx = unstriped(offs)
    idx2 = unstriped(offs2)
    idx3 = unstriped(offs3)
    idx4 = unstriped(offs4)
    keysu = unpack_weight(keys_words, keys_scales, "e2m1")
    keysidxg = keysu[:, idx]
    notesidx2q = mxq(f64(notes)[:, idx2], 0, "e4m3")
    g1 = keysidxg.T @ notesidx2q
    g0 = g1 * f64(given)[:, idx3]
    gr1 = g0 * f64(rowf)
    vt1 = f64(vals)[:, idx].T
    vt1q = mxq(vt1, 0, "e4m3")
    gr1q = mxq(gr1, 0, "e4m3")
    o = vt1q.T @ gr1q
    of = np.zeros((E, M))
    of[:, idx4] = o
    y = f64(old) + of
    words, scales = planes(y)
    return y, words, scales

@@ -1,0 +1,224 @@
+from contextlib import ExitStack
+
+import concourse.mybir as mybir
+from concourse.masks import make_identity
+
+D, T, I, J, U, Z, E, M = 512, 2048, 512, 512, 1024, 1024, 512, 1024
+FLOPS = 2 * D * I * J + 2 * I * E * J
+
+F32 = mybir.dt.float32
+BF16 = mybir.dt.bfloat16
+I32 = mybir.dt.int32
+U32 = mybir.dt.uint32
+U16 = mybir.dt.uint16
+U8 = mybir.dt.uint8
+FP8X4 = mybir.dt.float8_e4m3fn_x4
+FP4X4 = mybir.dt.float4_e2m1fn_x4
+COPY = mybir.ActivationFunctionType.Copy
+MULT = mybir.AluOpType.mult
+ADD = mybir.AluOpType.add
+
+P = 128
+PACK = 4
+LIST_COLS = I // 16
+
+
+def interleave(engine_copy, words, planes):
+    engine_copy(
+        out=words.rearrange("p (c i) t -> p c t i", i=4),
+        in_=planes.rearrange("p t (c i) -> p c t i", i=4),
+    )
+
+
+def tile_attend_tab_timestable_put_pl_kernel(
+    tc, keys_words, keys_scales, notes, given, rowf, vals, old, offs, offs2, offs3, offs4, out_0, out_1, out_2
+):
+    nc = tc.nc
+    with ExitStack() as ctx:
+        sb = ctx.enter_context(tc.tile_pool(name="sb", bufs=1))
+        ps = ctx.enter_context(tc.psum_pool(name="ps", bufs=1))
+        ps2 = ctx.enter_context(tc.psum_pool(name="ps2", bufs=2))
+
+        def tiles(name, shape, dtype):
+            return [sb.tile(shape, dtype, name="%s%d" % (name, t), align_bytes=64) for t in range(PACK)]
+
+        token_list = sb.tile([P, LIST_COLS], U16)
+        note_list = sb.tile([P, LIST_COLS], U16)
+        given_list = sb.tile([P, LIST_COLS], U16)
+        place_list = sb.tile([P, LIST_COLS], U16)
+        key_word_pool = sb.tile([P, T], U16, align_bytes=64)
+        key_scale_pool = sb.tile([P, T], U8, align_bytes=64)
+        note_pool = tiles("note_pool", [P, U], F32)
+        given_pool = tiles("given_pool", [P, Z], F32)
+        val_pool = tiles("val_pool", [P, T], F32)
+        placed = tiles("placed", [P, M], F32)
+        y = sb.tile([P, PACK, M], F32, align_bytes=64)
+        row_factor = sb.tile([P, PACK], F32)
+        identity = sb.tile([P, P], F32)
+
+        notes_by_place = notes.rearrange("(p t) u -> t p u", t=PACK)
+        given_by_place = given.rearrange("(p t) z -> t p z", t=PACK)
+        vals_by_place = vals.rearrange("(p t) c -> t p c", t=PACK)
+        old_by_place = old.rearrange("(p t) m -> t p m", t=PACK)
+        out_by_place = out_0.rearrange("(p t) m -> p t m", t=PACK)
+
+        nc.vector.memset(key_scale_pool[:].bitcast(I32), 0)
+        for q in range(4):
+            nc.gpsimd.dma_start(
+                out=key_scale_pool[32 * q : 32 * q + 4, :].bitcast(I32),
+                in_=keys_scales[0, 4 * q : 4 * q + 4, :].bitcast(I32),
+            )
+        nc.sync.dma_start(out=key_word_pool[:].bitcast(I32), in_=keys_words[0].bitcast(I32))
+        nc.sync.dma_start(out=note_pool[0][:], in_=notes_by_place[0])
+        nc.sync.dma_start(token_list[:], offs)
+        nc.sync.dma_start(note_list[:], offs2)
+        for t in range(1, PACK):
+            nc.sync.dma_start(out=note_pool[t][:], in_=notes_by_place[t])
+        nc.sync.dma_start(out=given_pool[0][:], in_=given_by_place[0])
+        nc.sync.dma_start(given_list[:], offs3)
+        nc.sync.dma_start(out=row_factor[:], in_=rowf.rearrange("(p t) o -> p (t o)", t=PACK))
+        for t in range(1, PACK):
+            nc.sync.dma_start(out=given_pool[t][:], in_=given_by_place[t])
+        nc.sync.dma_start(out=val_pool[0][:], in_=vals_by_place[0])
+        nc.sync.dma_start(place_list[:], offs4)
+        for t in range(1, PACK):
+            nc.sync.dma_start(out=val_pool[t][:], in_=vals_by_place[t])
+        for t in range(PACK):
+            nc.sync.dma_start(out=y[:, t, :], in_=old_by_place[t])
+
+        make_identity(nc, identity[:])
+        for t in range(PACK):
+            nc.vector.memset(placed[t][:], 0.0)
+
+        key_words_listed = sb.tile([P, I], U16, align_bytes=64)
+        key_words = sb.tile([P, PACK, P], U16, align_bytes=64)
+        key_scales = sb.tile([P, PACK, P], U8, align_bytes=64)
+        nc.vector.tensor_copy(key_words_listed[:], key_word_pool[:].indirect(token_list[:]))
+        nc.vector.tensor_copy(out=key_words[:], in_=key_words_listed[:].rearrange("p (s t) -> p t s", t=PACK))
+        nc.vector.tensor_copy(key_scales[:].rearrange("p t s -> p s t"), key_scale_pool[:].indirect(token_list[:]))
+
+        note_planes = sb.tile([P, PACK, J], BF16, align_bytes=64)
+        note_grouped = sb.tile([P, J, PACK], BF16, align_bytes=64)
+        note_codes = sb.tile([P, J], U32, align_bytes=64)
+        note_scales = sb.tile([P, J], U8, align_bytes=64)
+        for t in range(PACK):
+            nc.scalar.activation(note_planes[:, t, :], note_pool[t][:].indirect(note_list[:]), COPY)
+        interleave(nc.vector.tensor_copy, note_grouped[:], note_planes[:])
+        nc.vector.quantize_mx(
+            out=note_codes[:].bitcast(FP8X4), scales=note_scales[:], in_=note_grouped[:].rearrange("p j t -> p (j t)")
+        )
+
+        given_listed = tiles("given_listed", [P, J], F32)
+        table_planes = sb.tile([P, PACK, J], BF16, align_bytes=64)
+        table_grouped = sb.tile([P, J, PACK], BF16, align_bytes=64)
+        table_codes = sb.tile([P, J], U32, align_bytes=64)
+        table_scales = sb.tile([P, J], U8, align_bytes=64)
+        for t in range(PACK):
+            nc.scalar.activation(given_listed[t][:], given_pool[t][:].indirect(given_list[:]), COPY)
+            products = ps.tile([P, J], F32, name="products%d" % t)
+            nc.tensor.matmul_mx(
+                out=products[:],
+                lhsT=key_words[:, t, :].bitcast(FP4X4),
+                lhsT_scale=key_scales[:, t, :],
+                rhs=note_codes[:].bitcast(FP8X4),
+                rhs_scale=note_scales[:],
+                start=True,
+                stop=True,
+            )
+            nc.vector.scalar_tensor_tensor(
+                out=table_planes[:, t, :],
+                in0=products[:],
+                scalar=row_factor[:, t : t + 1],
+                in1=given_listed[t][:],
+                op0=MULT,
+                op1=MULT,
+            )
+        interleave(nc.vector.tensor_copy, table_grouped[:], table_planes[:])
+        nc.vector.quantize_mx(
+            out=table_codes[:].bitcast(FP8X4), scales=table_scales[:], in_=table_grouped[:].rearrange("p j t -> p (j t)")
+        )
+
+        vals_listed = tiles("vals_listed", [P, I], BF16)
+        val_grouped = tiles("val_grouped", [P, P, PACK], BF16)
+        val_codes = tiles("val_codes", [P, P], U32)
+        val_scales = tiles("val_scales", [P, P], U8)
+        sums = tiles("sums", [P, J], F32)
+
+        def prepare(r):
+            if r == 0:
+                nc.scalar.activation(vals_listed[r][:], val_pool[r][:].indirect(token_list[:]), COPY)
+            else:
+                nc.vector.tensor_copy(vals_listed[r][:], val_pool[r][:].indirect(token_list[:]))
+            pairs = vals_listed[r][:].bitcast(F32)
+            turned = ps2.tile([P, 2, P], F32, name="turned")
+            for u in range(2):
+                nc.tensor.transpose(turned[:, u, :], pairs[:, u : I // 2 : 2], identity[:])
+            copy = nc.scalar.copy if r == 0 else nc.vector.tensor_copy
+            copy(out=val_grouped[r][:].bitcast(F32), in_=turned[:].rearrange("p u e -> p e u"))
+            nc.vector.quantize_mx(
+                out=val_codes[r][:].bitcast(FP8X4),
+                scales=val_scales[r][:],
+                in_=val_grouped[r][:].rearrange("p e t -> p (e t)"),
+            )
+            acc = ps2.tile([P, J], F32, name="acc")
+            nc.tensor.matmul_mx(
+                out=acc[:],
+                lhsT=val_codes[r][:].bitcast(FP8X4),
+                lhsT_scale=val_scales[r][:],
+                rhs=table_codes[:].bitcast(FP8X4),
+                rhs_scale=table_scales[:],
+                start=True,
+                stop=True,
+            )
+            copy(out=sums[r][:], in_=acc[:])
+
+        def scatter(r):
+            if r == 2:
+                nc.vector.tensor_copy(placed[r][:].indirect(place_list[:]), sums[r][:])
+            else:
+                for h in range(2):
+                    nc.scalar.activation(
+                        placed[r][:].indirect(place_list[:, 16 * h : 16 * h + 16]),
+                        sums[r][:, 256 * h : 256 * h + 256],
+                        COPY,
+                    )
+
+        prepare(0)
+        scatter(0)
+        prepare(1)
+        scatter(1)
+        prepare(2)
+        prepare(3)
+        scatter(2)
+        scatter(3)
+        for r in range(2):
+            nc.gpsimd.tensor_tensor(out=y[:, r, :], in0=y[:, r, :], in1=placed[r][:], op=ADD)
+            nc.sync.dma_start(out=out_by_place[:, r, :], in_=y[:, r, :])
+
+        y_grouped = sb.tile([P, M, PACK], BF16, align_bytes=64)
+        y_codes = sb.tile([P, M], U32, align_bytes=64)
+        y_scales = sb.tile([P, M], U8, align_bytes=64)
+        words_out = out_1[0].rearrange("p m t -> p (m t)").bitcast(I32)
+        half = M // 2
+        nc.vector.tensor_tensor(out=y[:, 2, :], in0=y[:, 2, :], in1=placed[2][:], op=ADD)
+        nc.sync.dma_start(out=out_by_place[:, 2, :], in_=y[:, 2, :])
+        for h in range(2):
+            cols = slice(h * half, (h + 1) * half)
+            nc.vector.tensor_tensor(out=y[:, 3, cols], in0=y[:, 3, cols], in1=placed[3][:, cols], op=ADD)
+        nc.sync.dma_start(out=out_by_place[:, 3, :], in_=y[:, 3, :])
+        for h in range(2):
+            cols = slice(h * half, (h + 1) * half)
+            split = h * half + (384 if h == 0 else 128)
+            interleave(nc.scalar.copy, y_grouped[:, h * half : split, :], y[:, :, h * half : split])
+            interleave(nc.vector.tensor_copy, y_grouped[:, split : (h + 1) * half, :], y[:, :, split : (h + 1) * half])
+            nc.vector.quantize_mx(
+                out=y_codes[:, cols].bitcast(FP8X4),
+                scales=y_scales[:, cols],
+                in_=y_grouped[:, cols, :].rearrange("p m t -> p (m t)"),
+            )
+            nc.sync.dma_start(out=words_out[:, cols], in_=y_codes[:, cols].bitcast(I32))
+        for q in range(4):
+            queue = nc.sync if q % 2 == 0 else nc.scalar
+            queue.dma_start(
+                out=out_2[0, 4 * q : 4 * q + 4, :].bitcast(I32), in_=y_scales[32 * q : 32 * q + 4, :].bitcast(I32)
+            )

@@ -62,31 +62,41 @@ def tile_attend_tab_timestable_put_pl_kernel(
         old_by_place = old.rearrange("(p t) m -> t p m", t=PACK)
         out_by_place = out_0.rearrange("(p t) m -> p t m", t=PACK)
 
+        identity_bf16 = sb.tile([P, P], BF16)
+        make_identity(nc, identity_bf16[:])
+        nc.scalar.activation(identity[:], identity_bf16[:], COPY)
         nc.vector.memset(key_scale_pool[:].bitcast(I32), 0)
-        for q in range(4):
-            nc.gpsimd.dma_start(
+
+        def load_key_scales(q):
+            nc.sync.dma_start(
                 out=key_scale_pool[32 * q : 32 * q + 4, :].bitcast(I32),
                 in_=keys_scales[0, 4 * q : 4 * q + 4, :].bitcast(I32),
             )
-        nc.sync.dma_start(out=key_word_pool[:].bitcast(I32), in_=keys_words[0].bitcast(I32))
-        nc.sync.dma_start(out=note_pool[0][:], in_=notes_by_place[0])
-        nc.sync.dma_start(token_list[:], offs)
+
         nc.sync.dma_start(note_list[:], offs2)
-        for t in range(1, PACK):
-            nc.sync.dma_start(out=note_pool[t][:], in_=notes_by_place[t])
+        nc.sync.dma_start(token_list[:], offs)
+        nc.sync.dma_start(out=note_pool[0][:], in_=notes_by_place[0])
+        nc.sync.dma_start(out=key_word_pool[:].bitcast(I32), in_=keys_words[0].bitcast(I32))
+        nc.sync.dma_start(out=note_pool[1][:], in_=notes_by_place[1])
+        load_key_scales(0)
+        load_key_scales(1)
+        nc.sync.dma_start(out=note_pool[2][:], in_=notes_by_place[2])
+        load_key_scales(2)
+        load_key_scales(3)
+        nc.sync.dma_start(out=note_pool[3][:], in_=notes_by_place[3])
         nc.sync.dma_start(out=given_pool[0][:], in_=given_by_place[0])
         nc.sync.dma_start(given_list[:], offs3)
+        nc.sync.dma_start(out=given_pool[1][:], in_=given_by_place[1])
+        nc.sync.dma_start(out=given_pool[2][:], in_=given_by_place[2])
         nc.sync.dma_start(out=row_factor[:], in_=rowf.rearrange("(p t) o -> p (t o)", t=PACK))
-        for t in range(1, PACK):
-            nc.sync.dma_start(out=given_pool[t][:], in_=given_by_place[t])
+        nc.sync.dma_start(out=given_pool[3][:], in_=given_by_place[3])
         nc.sync.dma_start(out=val_pool[0][:], in_=vals_by_place[0])
         nc.sync.dma_start(place_list[:], offs4)
         for t in range(1, PACK):
             nc.sync.dma_start(out=val_pool[t][:], in_=vals_by_place[t])
-        for t in range(PACK):
+        for t in (0, 1, 3, 2):
             nc.sync.dma_start(out=y[:, t, :], in_=old_by_place[t])
 
-        make_identity(nc, identity[:])
         for t in range(PACK):
             nc.vector.memset(placed[t][:], 0.0)
 
@@ -95,21 +105,24 @@ def tile_attend_tab_timestable_put_pl_kernel(
         key_scales = sb.tile([P, PACK, P], U8, align_bytes=64)
         nc.vector.tensor_copy(key_words_listed[:], key_word_pool[:].indirect(token_list[:]))
         nc.vector.tensor_copy(out=key_words[:], in_=key_words_listed[:].rearrange("p (s t) -> p t s", t=PACK))
-        nc.vector.tensor_copy(key_scales[:].rearrange("p t s -> p s t"), key_scale_pool[:].indirect(token_list[:]))
+        key_scales_listed = sb.tile([P, I], U8, align_bytes=64)
+        nc.vector.tensor_copy(key_scales_listed[:], key_scale_pool[:].indirect(token_list[:]))
+        nc.vector.tensor_copy(out=key_scales[:], in_=key_scales_listed[:].rearrange("p (s t) -> p t s", t=PACK))
 
-        note_planes = sb.tile([P, PACK, J], BF16, align_bytes=64)
+        note_planes = sb.tile([P, PACK, J], F32, align_bytes=64)
         note_grouped = sb.tile([P, J, PACK], BF16, align_bytes=64)
         note_codes = sb.tile([P, J], U32, align_bytes=64)
         note_scales = sb.tile([P, J], U8, align_bytes=64)
-        for t in range(PACK):
+        for t in range(PACK - 1):
             nc.scalar.activation(note_planes[:, t, :], note_pool[t][:].indirect(note_list[:]), COPY)
+        nc.vector.tensor_copy(note_planes[:, PACK - 1, :], note_pool[PACK - 1][:].indirect(note_list[:]))
         interleave(nc.vector.tensor_copy, note_grouped[:], note_planes[:])
         nc.vector.quantize_mx(
             out=note_codes[:].bitcast(FP8X4), scales=note_scales[:], in_=note_grouped[:].rearrange("p j t -> p (j t)")
         )
 
         given_listed = tiles("given_listed", [P, J], F32)
-        table_planes = sb.tile([P, PACK, J], BF16, align_bytes=64)
+        table_planes = sb.tile([P, PACK, J], F32, align_bytes=64)
         table_grouped = sb.tile([P, J, PACK], BF16, align_bytes=64)
         table_codes = sb.tile([P, J], U32, align_bytes=64)
         table_scales = sb.tile([P, J], U8, align_bytes=64)
@@ -142,13 +155,15 @@ def tile_attend_tab_timestable_put_pl_kernel(
         val_grouped = tiles("val_grouped", [P, P, PACK], BF16)
         val_codes = tiles("val_codes", [P, P], U32)
         val_scales = tiles("val_scales", [P, P], U8)
-        sums = tiles("sums", [P, J], F32)
+        sums = {}
 
-        def prepare(r):
-            if r == 0:
+        def gather_vals(r):
+            if r < 2:
                 nc.scalar.activation(vals_listed[r][:], val_pool[r][:].indirect(token_list[:]), COPY)
             else:
                 nc.vector.tensor_copy(vals_listed[r][:], val_pool[r][:].indirect(token_list[:]))
+
+        def prepare(r):
             pairs = vals_listed[r][:].bitcast(F32)
             turned = ps2.tile([P, 2, P], F32, name="turned")
             for u in range(2):
@@ -170,10 +185,16 @@ def tile_attend_tab_timestable_put_pl_kernel(
                 start=True,
                 stop=True,
             )
+            return acc
+
+        def empty(r, acc):
+            tag = "val_pool%d" % (r + 1) if r + 1 < PACK else "sums%d" % r
+            sums[r] = sb.tile([P, J], F32, name="sums%d" % r, tag=tag, align_bytes=64)
+            copy = nc.scalar.copy if r == 0 else nc.vector.tensor_copy
             copy(out=sums[r][:], in_=acc[:])
 
         def scatter(r):
-            if r == 2:
+            if r == 3:
                 nc.vector.tensor_copy(placed[r][:].indirect(place_list[:]), sums[r][:])
             else:
                 for h in range(2):
@@ -183,14 +204,15 @@ def tile_attend_tab_timestable_put_pl_kernel(
                         COPY,
                     )
 
-        prepare(0)
-        scatter(0)
-        prepare(1)
-        scatter(1)
-        prepare(2)
-        prepare(3)
-        scatter(2)
-        scatter(3)
+        gather_vals(0)
+        banks = [prepare(0)]
+        for r in range(PACK):
+            if r + 1 < PACK:
+                gather_vals(r + 1)
+            empty(r, banks[r])
+            if r + 1 < PACK:
+                banks.append(prepare(r + 1))
+            scatter(r)
         for r in range(2):
             nc.gpsimd.tensor_tensor(out=y[:, r, :], in0=y[:, r, :], in1=placed[r][:], op=ADD)
             nc.sync.dma_start(out=out_by_place[:, r, :], in_=y[:, r, :])
@@ -199,18 +221,19 @@ def tile_attend_tab_timestable_put_pl_kernel(
         y_codes = sb.tile([P, M], U32, align_bytes=64)
         y_scales = sb.tile([P, M], U8, align_bytes=64)
         words_out = out_1[0].rearrange("p m t -> p (m t)").bitcast(I32)
-        half = M // 2
-        nc.vector.tensor_tensor(out=y[:, 2, :], in0=y[:, 2, :], in1=placed[2][:], op=ADD)
-        nc.sync.dma_start(out=out_by_place[:, 2, :], in_=y[:, 2, :])
-        for h in range(2):
-            cols = slice(h * half, (h + 1) * half)
-            nc.vector.tensor_tensor(out=y[:, 3, cols], in0=y[:, 3, cols], in1=placed[3][:, cols], op=ADD)
+        nc.vector.tensor_tensor(out=y[:, 3, :], in0=y[:, 3, :], in1=placed[3][:], op=ADD)
         nc.sync.dma_start(out=out_by_place[:, 3, :], in_=y[:, 3, :])
-        for h in range(2):
-            cols = slice(h * half, (h + 1) * half)
-            split = h * half + (384 if h == 0 else 128)
-            interleave(nc.scalar.copy, y_grouped[:, h * half : split, :], y[:, :, h * half : split])
-            interleave(nc.vector.tensor_copy, y_grouped[:, split : (h + 1) * half, :], y[:, :, split : (h + 1) * half])
+        quarter = M // 4
+        for c in range(4):
+            cols = slice(c * quarter, (c + 1) * quarter)
+            nc.vector.tensor_tensor(out=y[:, 2, cols], in0=y[:, 2, cols], in1=placed[2][:, cols], op=ADD)
+        nc.sync.dma_start(out=out_by_place[:, 2, :], in_=y[:, 2, :])
+        split = 640
+        for lo, hi in ((0, 256), (256, 512), (512, split)):
+            interleave(nc.scalar.copy, y_grouped[:, lo:hi, :], y[:, :, lo:hi])
+        interleave(nc.vector.tensor_copy, y_grouped[:, split:M, :], y[:, :, split:M])
+        for c in (0, 3, 1, 2):
+            cols = slice(c * quarter, (c + 1) * quarter)
             nc.vector.quantize_mx(
                 out=y_codes[:, cols].bitcast(FP8X4),
                 scales=y_scales[:, cols],

@@ -52,7 +52,7 @@ def tile_attend_tab_timestable_put_pl_kernel(
         given_pool = tiles("given_pool", [P, Z], F32)
         val_pool = tiles("val_pool", [P, T], F32)
         placed = tiles("placed", [P, M], F32)
-        y = sb.tile([P, PACK, M], F32, align_bytes=64)
+        old_rows = sb.tile([P, PACK, M], F32, align_bytes=64)
         row_factor = sb.tile([P, PACK], F32)
         identity = sb.tile([P, P], F32)
 
@@ -62,14 +62,13 @@ def tile_attend_tab_timestable_put_pl_kernel(
         old_by_place = old.rearrange("(p t) m -> t p m", t=PACK)
         out_by_place = out_0.rearrange("(p t) m -> p t m", t=PACK)
 
-        identity_bf16 = sb.tile([P, P], BF16)
-        make_identity(nc, identity_bf16[:])
-        nc.scalar.activation(identity[:], identity_bf16[:], COPY)
+        make_identity(nc, identity[:])
         nc.vector.memset(key_scale_pool[:].bitcast(I32), 0)
+        key_scale_rows = sb.tile([P, T // 4], I32, align_bytes=64)
 
         def load_key_scales(q):
             nc.sync.dma_start(
-                out=key_scale_pool[32 * q : 32 * q + 4, :].bitcast(I32),
+                out=key_scale_rows[32 * q : 32 * q + 4, :],
                 in_=keys_scales[0, 4 * q : 4 * q + 4, :].bitcast(I32),
             )
 
@@ -94,17 +93,21 @@ def tile_attend_tab_timestable_put_pl_kernel(
         nc.sync.dma_start(place_list[:], offs4)
         for t in range(1, PACK):
             nc.sync.dma_start(out=val_pool[t][:], in_=vals_by_place[t])
-        for t in (0, 1, 3, 2):
-            nc.sync.dma_start(out=y[:, t, :], in_=old_by_place[t])
+        for t in range(PACK):
+            nc.sync.dma_start(out=old_rows[:, t, :], in_=old_by_place[t])
 
         for t in range(PACK):
-            nc.vector.memset(placed[t][:], 0.0)
+            engine = nc.vector if t < 2 else nc.gpsimd
+            engine.memset(placed[t][:], 0.0)
 
         key_words_listed = sb.tile([P, I], U16, align_bytes=64)
         key_words = sb.tile([P, PACK, P], U16, align_bytes=64)
         key_scales = sb.tile([P, PACK, P], U8, align_bytes=64)
         nc.vector.tensor_copy(key_words_listed[:], key_word_pool[:].indirect(token_list[:]))
         nc.vector.tensor_copy(out=key_words[:], in_=key_words_listed[:].rearrange("p (s t) -> p t s", t=PACK))
+        for q in range(4):
+            rows = slice(32 * q, 32 * q + 4)
+            nc.vector.tensor_copy(out=key_scale_pool[rows, :].bitcast(I32), in_=key_scale_rows[rows, :])
         key_scales_listed = sb.tile([P, I], U8, align_bytes=64)
         nc.vector.tensor_copy(key_scales_listed[:], key_scale_pool[:].indirect(token_list[:]))
         nc.vector.tensor_copy(out=key_scales[:], in_=key_scales_listed[:].rearrange("p (s t) -> p t s", t=PACK))
@@ -113,9 +116,8 @@ def tile_attend_tab_timestable_put_pl_kernel(
         note_grouped = sb.tile([P, J, PACK], BF16, align_bytes=64)
         note_codes = sb.tile([P, J], U32, align_bytes=64)
         note_scales = sb.tile([P, J], U8, align_bytes=64)
-        for t in range(PACK - 1):
+        for t in range(PACK):
             nc.scalar.activation(note_planes[:, t, :], note_pool[t][:].indirect(note_list[:]), COPY)
-        nc.vector.tensor_copy(note_planes[:, PACK - 1, :], note_pool[PACK - 1][:].indirect(note_list[:]))
         interleave(nc.vector.tensor_copy, note_grouped[:], note_planes[:])
         nc.vector.quantize_mx(
             out=note_codes[:].bitcast(FP8X4), scales=note_scales[:], in_=note_grouped[:].rearrange("p j t -> p (j t)")
@@ -126,8 +128,9 @@ def tile_attend_tab_timestable_put_pl_kernel(
         table_grouped = sb.tile([P, J, PACK], BF16, align_bytes=64)
         table_codes = sb.tile([P, J], U32, align_bytes=64)
         table_scales = sb.tile([P, J], U8, align_bytes=64)
+        halves = [slice(0, J // 2), slice(J // 2, J)]
+        list_halves = [slice(0, LIST_COLS // 2), slice(LIST_COLS // 2, LIST_COLS)]
         for t in range(PACK):
-            nc.scalar.activation(given_listed[t][:], given_pool[t][:].indirect(given_list[:]), COPY)
             products = ps.tile([P, J], F32, name="products%d" % t)
             nc.tensor.matmul_mx(
                 out=products[:],
@@ -138,24 +141,29 @@ def tile_attend_tab_timestable_put_pl_kernel(
                 start=True,
                 stop=True,
             )
-            nc.vector.scalar_tensor_tensor(
-                out=table_planes[:, t, :],
-                in0=products[:],
-                scalar=row_factor[:, t : t + 1],
-                in1=given_listed[t][:],
-                op0=MULT,
-                op1=MULT,
+            pieces = zip(halves, list_halves) if t == PACK - 1 else [(slice(0, J), slice(0, LIST_COLS))]
+            for cols, entries in pieces:
+                nc.scalar.activation(given_listed[t][:, cols], given_pool[t][:].indirect(given_list[:, entries]), COPY)
+                nc.vector.scalar_tensor_tensor(
+                    out=table_planes[:, t, cols],
+                    in0=products[:, cols],
+                    scalar=row_factor[:, t : t + 1],
+                    in1=given_listed[t][:, cols],
+                    op0=MULT,
+                    op1=MULT,
+                )
+        for cols in halves:
+            interleave(nc.vector.tensor_copy, table_grouped[:, cols, :], table_planes[:, :, cols])
+        for cols in halves:
+            nc.vector.quantize_mx(
+                out=table_codes[:, cols].bitcast(FP8X4),
+                scales=table_scales[:, cols],
+                in_=table_grouped[:, cols, :].rearrange("p j t -> p (j t)"),
             )
-        interleave(nc.vector.tensor_copy, table_grouped[:], table_planes[:])
-        nc.vector.quantize_mx(
-            out=table_codes[:].bitcast(FP8X4), scales=table_scales[:], in_=table_grouped[:].rearrange("p j t -> p (j t)")
-        )
 
         vals_listed = tiles("vals_listed", [P, I], BF16)
-        val_grouped = tiles("val_grouped", [P, P, PACK], BF16)
         val_codes = tiles("val_codes", [P, P], U32)
         val_scales = tiles("val_scales", [P, P], U8)
-        sums = {}
 
         def gather_vals(r):
             if r < 2:
@@ -168,71 +176,85 @@ def tile_attend_tab_timestable_put_pl_kernel(
             turned = ps2.tile([P, 2, P], F32, name="turned")
             for u in range(2):
                 nc.tensor.transpose(turned[:, u, :], pairs[:, u : I // 2 : 2], identity[:])
+            tag = "val_pool%d" % (r + 1) if r in (1, 2) else "val_grouped%d" % r
+            grouped = sb.tile([P, P, PACK], BF16, name="val_grouped%d" % r, tag=tag, align_bytes=64)
             copy = nc.scalar.copy if r == 0 else nc.vector.tensor_copy
-            copy(out=val_grouped[r][:].bitcast(F32), in_=turned[:].rearrange("p u e -> p e u"))
+            copy(out=grouped[:].bitcast(F32), in_=turned[:].rearrange("p u e -> p e u"))
             nc.vector.quantize_mx(
                 out=val_codes[r][:].bitcast(FP8X4),
                 scales=val_scales[r][:],
-                in_=val_grouped[r][:].rearrange("p e t -> p (e t)"),
+                in_=grouped[:].rearrange("p e t -> p (e t)"),
             )
-            acc = ps2.tile([P, J], F32, name="acc")
+
+        def multiply(r, bank, cols):
             nc.tensor.matmul_mx(
-                out=acc[:],
+                out=bank[:],
                 lhsT=val_codes[r][:].bitcast(FP8X4),
                 lhsT_scale=val_scales[r][:],
-                rhs=table_codes[:].bitcast(FP8X4),
-                rhs_scale=table_scales[:],
+                rhs=table_codes[:, cols].bitcast(FP8X4),
+                rhs_scale=table_scales[:, cols],
                 start=True,
                 stop=True,
             )
-            return acc
 
-        def empty(r, acc):
-            tag = "val_pool%d" % (r + 1) if r + 1 < PACK else "sums%d" % r
-            sums[r] = sb.tile([P, J], F32, name="sums%d" % r, tag=tag, align_bytes=64)
-            copy = nc.scalar.copy if r == 0 else nc.vector.tensor_copy
-            copy(out=sums[r][:], in_=acc[:])
-
-        def scatter(r):
-            if r == 3:
-                nc.vector.tensor_copy(placed[r][:].indirect(place_list[:]), sums[r][:])
-            else:
-                for h in range(2):
-                    nc.scalar.activation(
-                        placed[r][:].indirect(place_list[:, 16 * h : 16 * h + 16]),
-                        sums[r][:, 256 * h : 256 * h + 256],
-                        COPY,
-                    )
+        def scatter_on_scalar(r, h, source):
+            nc.scalar.activation(placed[r][:].indirect(place_list[:, list_halves[h]]), source, COPY)
 
         gather_vals(0)
-        banks = [prepare(0)]
-        for r in range(PACK):
-            if r + 1 < PACK:
-                gather_vals(r + 1)
-            empty(r, banks[r])
-            if r + 1 < PACK:
-                banks.append(prepare(r + 1))
-            scatter(r)
-        for r in range(2):
-            nc.gpsimd.tensor_tensor(out=y[:, r, :], in0=y[:, r, :], in1=placed[r][:], op=ADD)
+        prepare(0)
+        gather_vals(1)
+        sums = sb.tile([P, J], F32, name="sums0", tag="val_pool1", align_bytes=64)
+        for h in range(2):
+            bank = ps.tile([P, J // 2], F32, name="half_sums%d" % h, tag="products%d" % h)
+            multiply(0, bank, halves[h])
+            nc.scalar.copy(out=sums[:, halves[h]], in_=bank[:])
+            scatter_on_scalar(0, h, sums[:, halves[h]])
+        gather_vals(2)
+        prepare(1)
+        bank = ps2.tile([P, J], F32, name="acc")
+        multiply(1, bank, slice(0, J))
+        sums = sb.tile([P, J], F32, name="sums1", align_bytes=64)
+        nc.scalar.copy(out=sums[:], in_=bank[:])
+        for h in range(2):
+            scatter_on_scalar(1, h, sums[:, halves[h]])
+        gather_vals(3)
+        prepare(2)
+        prepare(3)
+        bank = ps2.tile([P, J], F32, name="acc")
+        multiply(2, bank, slice(0, J))
+        sums = sb.tile([P, J], F32, name="sums2", tag="val_grouped3", align_bytes=64)
+        nc.vector.tensor_copy(out=sums[:], in_=bank[:])
+        for h in range(2):
+            scatter_on_scalar(2, h, sums[:, halves[h]])
+        bank = ps2.tile([P, J], F32, name="acc")
+        multiply(3, bank, slice(0, J))
+        share = 384
+        sums_vector = sb.tile([P, share], F32, align_bytes=64)
+        sums_scalar = sb.tile([P, J - share], F32, align_bytes=64)
+        nc.vector.tensor_copy(out=sums_vector[:], in_=bank[:, 0:share])
+        nc.vector.tensor_copy(out=sums_scalar[:], in_=bank[:, share:J])
+        nc.vector.tensor_copy(placed[3][:].indirect(place_list[:, 0 : share // 16]), sums_vector[:])
+        nc.scalar.activation(placed[3][:].indirect(place_list[:, share // 16 : LIST_COLS]), sums_scalar[:], COPY)
+
+        y = sb.tile([P, PACK, M], F32, tag="sums_vector", align_bytes=64)
+        for r in range(3):
+            nc.vector.tensor_tensor(out=y[:, r, :], in0=old_rows[:, r, :], in1=placed[r][:], op=ADD)
             nc.sync.dma_start(out=out_by_place[:, r, :], in_=y[:, r, :])
 
         y_grouped = sb.tile([P, M, PACK], BF16, align_bytes=64)
         y_codes = sb.tile([P, M], U32, align_bytes=64)
         y_scales = sb.tile([P, M], U8, align_bytes=64)
         words_out = out_1[0].rearrange("p m t -> p (m t)").bitcast(I32)
-        nc.vector.tensor_tensor(out=y[:, 3, :], in0=y[:, 3, :], in1=placed[3][:], op=ADD)
-        nc.sync.dma_start(out=out_by_place[:, 3, :], in_=y[:, 3, :])
         quarter = M // 4
         for c in range(4):
             cols = slice(c * quarter, (c + 1) * quarter)
-            nc.vector.tensor_tensor(out=y[:, 2, cols], in0=y[:, 2, cols], in1=placed[2][:, cols], op=ADD)
-        nc.sync.dma_start(out=out_by_place[:, 2, :], in_=y[:, 2, :])
-        split = 640
-        for lo, hi in ((0, 256), (256, 512), (512, split)):
+            nc.vector.tensor_tensor(out=y[:, 3, cols], in0=old_rows[:, 3, cols], in1=placed[3][:, cols], op=ADD)
+        nc.sync.dma_start(out=out_by_place[:, 3, :], in_=y[:, 3, :])
+        split = 512
+        for lo, hi in ((0, 256), (256, split)):
             interleave(nc.scalar.copy, y_grouped[:, lo:hi, :], y[:, :, lo:hi])
         interleave(nc.vector.tensor_copy, y_grouped[:, split:M, :], y[:, :, split:M])
-        for c in (0, 3, 1, 2):
+        for c in (0, 2, 3, 1):
             cols = slice(c * quarter, (c + 1) * quarter)
             nc.vector.quantize_mx(
                 out=y_codes[:, cols].bitcast(FP8X4),

@@ -37,7 +37,6 @@ def tile_attend_tab_timestable_put_pl_kernel(
     with ExitStack() as ctx:
         sb = ctx.enter_context(tc.tile_pool(name="sb", bufs=1))
         ps = ctx.enter_context(tc.psum_pool(name="ps", bufs=1))
-        ps2 = ctx.enter_context(tc.psum_pool(name="ps2", bufs=2))
 
         def tiles(name, shape, dtype):
             return [sb.tile(shape, dtype, name="%s%d" % (name, t), align_bytes=64) for t in range(PACK)]
@@ -52,7 +51,7 @@ def tile_attend_tab_timestable_put_pl_kernel(
         given_pool = tiles("given_pool", [P, Z], F32)
         val_pool = tiles("val_pool", [P, T], F32)
         placed = tiles("placed", [P, M], F32)
-        old_rows = sb.tile([P, PACK, M], F32, align_bytes=64)
+        old_rows = sb.tile([P, PACK - 1, M], F32, align_bytes=64)
         row_factor = sb.tile([P, PACK], F32)
         identity = sb.tile([P, P], F32)
 
@@ -93,7 +92,7 @@ def tile_attend_tab_timestable_put_pl_kernel(
         nc.sync.dma_start(place_list[:], offs4)
         for t in range(1, PACK):
             nc.sync.dma_start(out=val_pool[t][:], in_=vals_by_place[t])
-        for t in range(PACK):
+        for t in range(PACK - 1):
             nc.sync.dma_start(out=old_rows[:, t, :], in_=old_by_place[t])
 
         for t in range(PACK):
@@ -116,16 +115,41 @@ def tile_attend_tab_timestable_put_pl_kernel(
         note_grouped = sb.tile([P, J, PACK], BF16, align_bytes=64)
         note_codes = sb.tile([P, J], U32, align_bytes=64)
         note_scales = sb.tile([P, J], U8, align_bytes=64)
-        for t in range(PACK):
+        for t in range(PACK - 1):
             nc.scalar.activation(note_planes[:, t, :], note_pool[t][:].indirect(note_list[:]), COPY)
+        nc.vector.tensor_copy(note_planes[:, PACK - 1, :], note_pool[PACK - 1][:].indirect(note_list[:]))
         interleave(nc.vector.tensor_copy, note_grouped[:], note_planes[:])
         nc.vector.quantize_mx(
             out=note_codes[:].bitcast(FP8X4), scales=note_scales[:], in_=note_grouped[:].rearrange("p j t -> p (j t)")
         )
 
+        vals_listed = tiles("vals_listed", [P, I], BF16)
+        val_codes = tiles("val_codes", [P, P], U32)
+        val_scales = tiles("val_scales", [P, P], U8)
+
+        def gather_vals(r):
+            if r < 2:
+                nc.scalar.activation(vals_listed[r][:], val_pool[r][:].indirect(token_list[:]), COPY)
+            else:
+                nc.vector.tensor_copy(vals_listed[r][:], val_pool[r][:].indirect(token_list[:]))
+
+        def prepare(r):
+            pairs = vals_listed[r][:].bitcast(F32)
+            turned = ps.tile([P, 2, P], F32, name="turned%d" % r, tag="turned%d" % (r % 2))
+            for u in range(2):
+                nc.tensor.transpose(turned[:, u, :], pairs[:, u : I // 2 : 2], identity[:])
+            tag = "val_pool%d" % (r + 1) if r in (1, 2) else "val_grouped%d" % r
+            grouped = sb.tile([P, P, PACK], BF16, name="val_grouped%d" % r, tag=tag, align_bytes=64)
+            copy = nc.scalar.copy if r == 0 else nc.vector.tensor_copy
+            copy(out=grouped[:].bitcast(F32), in_=turned[:].rearrange("p u e -> p e u"))
+            nc.vector.quantize_mx(
+                out=val_codes[r][:].bitcast(FP8X4),
+                scales=val_scales[r][:],
+                in_=grouped[:].rearrange("p e t -> p (e t)"),
+            )
+
         given_listed = tiles("given_listed", [P, J], F32)
         table_planes = sb.tile([P, PACK, J], F32, align_bytes=64)
-        table_grouped = sb.tile([P, J, PACK], BF16, align_bytes=64)
         table_codes = sb.tile([P, J], U32, align_bytes=64)
         table_scales = sb.tile([P, J], U8, align_bytes=64)
         halves = [slice(0, J // 2), slice(J // 2, J)]
@@ -141,49 +165,23 @@ def tile_attend_tab_timestable_put_pl_kernel(
                 start=True,
                 stop=True,
             )
-            pieces = zip(halves, list_halves) if t == PACK - 1 else [(slice(0, J), slice(0, LIST_COLS))]
-            for cols, entries in pieces:
-                nc.scalar.activation(given_listed[t][:, cols], given_pool[t][:].indirect(given_list[:, entries]), COPY)
-                nc.vector.scalar_tensor_tensor(
-                    out=table_planes[:, t, cols],
-                    in0=products[:, cols],
-                    scalar=row_factor[:, t : t + 1],
-                    in1=given_listed[t][:, cols],
-                    op0=MULT,
-                    op1=MULT,
-                )
-        for cols in halves:
-            interleave(nc.vector.tensor_copy, table_grouped[:, cols, :], table_planes[:, :, cols])
-        for cols in halves:
-            nc.vector.quantize_mx(
-                out=table_codes[:, cols].bitcast(FP8X4),
-                scales=table_scales[:, cols],
-                in_=table_grouped[:, cols, :].rearrange("p j t -> p (j t)"),
+            nc.scalar.activation(given_listed[t][:], given_pool[t][:].indirect(given_list[:]), COPY)
+            nc.vector.scalar_tensor_tensor(
+                out=table_planes[:, t, :],
+                in0=products[:],
+                scalar=row_factor[:, t : t + 1],
+                in1=given_listed[t][:],
+                op0=MULT,
+                op1=MULT,
             )
 
-        vals_listed = tiles("vals_listed", [P, I], BF16)
-        val_codes = tiles("val_codes", [P, P], U32)
-        val_scales = tiles("val_scales", [P, P], U8)
-
-        def gather_vals(r):
-            if r < 2:
-                nc.scalar.activation(vals_listed[r][:], val_pool[r][:].indirect(token_list[:]), COPY)
-            else:
-                nc.vector.tensor_copy(vals_listed[r][:], val_pool[r][:].indirect(token_list[:]))
-
-        def prepare(r):
-            pairs = vals_listed[r][:].bitcast(F32)
-            turned = ps2.tile([P, 2, P], F32, name="turned")
-            for u in range(2):
-                nc.tensor.transpose(turned[:, u, :], pairs[:, u : I // 2 : 2], identity[:])
-            tag = "val_pool%d" % (r + 1) if r in (1, 2) else "val_grouped%d" % r
-            grouped = sb.tile([P, P, PACK], BF16, name="val_grouped%d" % r, tag=tag, align_bytes=64)
-            copy = nc.scalar.copy if r == 0 else nc.vector.tensor_copy
-            copy(out=grouped[:].bitcast(F32), in_=turned[:].rearrange("p u e -> p e u"))
+        def quantise_table(h, tag):
+            grouped = sb.tile([P, J // 2, PACK], BF16, name="table_grouped%d" % h, tag=tag, align_bytes=64)
+            interleave(nc.vector.tensor_copy, grouped[:], table_planes[:, :, halves[h]])
             nc.vector.quantize_mx(
-                out=val_codes[r][:].bitcast(FP8X4),
-                scales=val_scales[r][:],
-                in_=grouped[:].rearrange("p e t -> p (e t)"),
+                out=table_codes[:, halves[h]].bitcast(FP8X4),
+                scales=table_scales[:, halves[h]],
+                in_=grouped[:].rearrange("p j t -> p (j t)"),
             )
 
         def multiply(r, bank, cols):
@@ -200,18 +198,20 @@ def tile_attend_tab_timestable_put_pl_kernel(
         def scatter_on_scalar(r, h, source):
             nc.scalar.activation(placed[r][:].indirect(place_list[:, list_halves[h]]), source, COPY)
 
+        quantise_table(0, "table_grouped0")
         gather_vals(0)
         prepare(0)
+        quantise_table(1, "val_grouped0")
         gather_vals(1)
-        sums = sb.tile([P, J], F32, name="sums0", tag="val_pool1", align_bytes=64)
         for h in range(2):
+            sums = sb.tile([P, J // 2], F32, name="sums0_%d" % h, tag="val_pool1", align_bytes=64)
             bank = ps.tile([P, J // 2], F32, name="half_sums%d" % h, tag="products%d" % h)
             multiply(0, bank, halves[h])
-            nc.scalar.copy(out=sums[:, halves[h]], in_=bank[:])
-            scatter_on_scalar(0, h, sums[:, halves[h]])
+            nc.scalar.copy(out=sums[:], in_=bank[:])
+            scatter_on_scalar(0, h, sums[:])
         gather_vals(2)
         prepare(1)
-        bank = ps2.tile([P, J], F32, name="acc")
+        bank = ps.tile([P, J], F32, name="bank1")
         multiply(1, bank, slice(0, J))
         sums = sb.tile([P, J], F32, name="sums1", align_bytes=64)
         nc.scalar.copy(out=sums[:], in_=bank[:])
@@ -220,25 +220,22 @@ def tile_attend_tab_timestable_put_pl_kernel(
         gather_vals(3)
         prepare(2)
         prepare(3)
-        bank = ps2.tile([P, J], F32, name="acc")
+        bank = ps.tile([P, J], F32, name="bank2", tag="turned1")
         multiply(2, bank, slice(0, J))
-        sums = sb.tile([P, J], F32, name="sums2", tag="val_grouped3", align_bytes=64)
+        sums = sb.tile([P, J], F32, name="sums2", align_bytes=64)
         nc.vector.tensor_copy(out=sums[:], in_=bank[:])
         for h in range(2):
             scatter_on_scalar(2, h, sums[:, halves[h]])
-        bank = ps2.tile([P, J], F32, name="acc")
+        bank = ps.tile([P, J], F32, name="bank3")
         multiply(3, bank, slice(0, J))
-        share = 384
-        sums_vector = sb.tile([P, share], F32, align_bytes=64)
-        sums_scalar = sb.tile([P, J - share], F32, align_bytes=64)
-        nc.vector.tensor_copy(out=sums_vector[:], in_=bank[:, 0:share])
-        nc.vector.tensor_copy(out=sums_scalar[:], in_=bank[:, share:J])
-        nc.vector.tensor_copy(placed[3][:].indirect(place_list[:, 0 : share // 16]), sums_vector[:])
-        nc.scalar.activation(placed[3][:].indirect(place_list[:, share // 16 : LIST_COLS]), sums_scalar[:], COPY)
+        sums = sb.tile([P, J], F32, name="sums3", align_bytes=64)
+        nc.vector.tensor_copy(out=sums[:], in_=bank[:])
+        nc.vector.tensor_copy(placed[3][:].indirect(place_list[:]), sums[:])
 
-        y = sb.tile([P, PACK, M], F32, tag="sums_vector", align_bytes=64)
-        for r in range(3):
-            nc.vector.tensor_tensor(out=y[:, r, :], in0=old_rows[:, r, :], in1=placed[r][:], op=ADD)
+        y = sb.tile([P, PACK, M], F32, tag="val_grouped3", align_bytes=64)
+        nc.sync.dma_start(out=y[:, 2, :], in_=old_by_place[3])
+        for r in range(2):
+            nc.gpsimd.tensor_tensor(out=y[:, r, :], in0=old_rows[:, r, :], in1=placed[r][:], op=ADD)
             nc.sync.dma_start(out=out_by_place[:, r, :], in_=y[:, r, :])
 
         y_grouped = sb.tile([P, M, PACK], BF16, align_bytes=64)
@@ -246,15 +243,17 @@ def tile_attend_tab_timestable_put_pl_kernel(
         y_scales = sb.tile([P, M], U8, align_bytes=64)
         words_out = out_1[0].rearrange("p m t -> p (m t)").bitcast(I32)
         quarter = M // 4
+        nc.vector.tensor_tensor(out=y[:, 3, :], in0=y[:, 2, :], in1=placed[3][:], op=ADD)
+        nc.sync.dma_start(out=out_by_place[:, 3, :], in_=y[:, 3, :])
         for c in range(4):
             cols = slice(c * quarter, (c + 1) * quarter)
-            nc.vector.tensor_tensor(out=y[:, 3, cols], in0=old_rows[:, 3, cols], in1=placed[3][:, cols], op=ADD)
-        nc.sync.dma_start(out=out_by_place[:, 3, :], in_=y[:, 3, :])
-        split = 512
-        for lo, hi in ((0, 256), (256, split)):
+            nc.vector.tensor_tensor(out=y[:, 2, cols], in0=old_rows[:, 2, cols], in1=placed[2][:, cols], op=ADD)
+        nc.sync.dma_start(out=out_by_place[:, 2, :], in_=y[:, 2, :])
+        split = 608
+        for lo, hi in ((0, 256), (256, 512), (512, split)):
             interleave(nc.scalar.copy, y_grouped[:, lo:hi, :], y[:, :, lo:hi])
         interleave(nc.vector.tensor_copy, y_grouped[:, split:M, :], y[:, :, split:M])
-        for c in (0, 2, 3, 1):
+        for c in (0, 3, 1, 2):
             cols = slice(c * quarter, (c + 1) * quarter)
             nc.vector.quantize_mx(
                 out=y_codes[:, cols].bitcast(FP8X4),

@@ -20,12 +20,14 @@ ADD = mybir.AluOpType.add
 
 P = 128
 PACK = 4
+QUADRANTS = 4
 LIST_COLS = I // 16
+LAST = PACK - 1
 
 
-def interleave(engine_copy, words, planes):
+def interleave(engine_copy, grouped, planes):
     engine_copy(
-        out=words.rearrange("p (c i) t -> p c t i", i=4),
+        out=grouped.rearrange("p (c i) t -> p c t i", i=4),
         in_=planes.rearrange("p t (c i) -> p c t i", i=4),
     )
 
@@ -51,7 +53,7 @@ def tile_attend_tab_timestable_put_pl_kernel(
         given_pool = tiles("given_pool", [P, Z], F32)
         val_pool = tiles("val_pool", [P, T], F32)
         placed = tiles("placed", [P, M], F32)
-        old_rows = sb.tile([P, PACK - 1, M], F32, align_bytes=64)
+        old_rows = sb.tile([P, LAST, M], F32, align_bytes=64)
         row_factor = sb.tile([P, PACK], F32)
         identity = sb.tile([P, P], F32)
 
@@ -90,21 +92,21 @@ def tile_attend_tab_timestable_put_pl_kernel(
         nc.sync.dma_start(out=given_pool[3][:], in_=given_by_place[3])
         nc.sync.dma_start(out=val_pool[0][:], in_=vals_by_place[0])
         nc.sync.dma_start(place_list[:], offs4)
-        for t in range(1, PACK):
-            nc.sync.dma_start(out=val_pool[t][:], in_=vals_by_place[t])
-        for t in range(PACK - 1):
-            nc.sync.dma_start(out=old_rows[:, t, :], in_=old_by_place[t])
+        for r in range(1, PACK):
+            nc.sync.dma_start(out=val_pool[r][:], in_=vals_by_place[r])
+        for r in range(LAST):
+            nc.sync.dma_start(out=old_rows[:, r, :], in_=old_by_place[r])
 
-        for t in range(PACK):
-            engine = nc.vector if t < 2 else nc.gpsimd
-            engine.memset(placed[t][:], 0.0)
+        for r in range(PACK):
+            engine = nc.vector if r < 2 else nc.gpsimd
+            engine.memset(placed[r][:], 0.0)
 
         key_words_listed = sb.tile([P, I], U16, align_bytes=64)
         key_words = sb.tile([P, PACK, P], U16, align_bytes=64)
         key_scales = sb.tile([P, PACK, P], U8, align_bytes=64)
         nc.vector.tensor_copy(key_words_listed[:], key_word_pool[:].indirect(token_list[:]))
         nc.vector.tensor_copy(out=key_words[:], in_=key_words_listed[:].rearrange("p (s t) -> p t s", t=PACK))
-        for q in range(4):
+        for q in range(QUADRANTS):
             rows = slice(32 * q, 32 * q + 4)
             nc.vector.tensor_copy(out=key_scale_pool[rows, :].bitcast(I32), in_=key_scale_rows[rows, :])
         key_scales_listed = sb.tile([P, I], U8, align_bytes=64)
@@ -115,41 +117,16 @@ def tile_attend_tab_timestable_put_pl_kernel(
         note_grouped = sb.tile([P, J, PACK], BF16, align_bytes=64)
         note_codes = sb.tile([P, J], U32, align_bytes=64)
         note_scales = sb.tile([P, J], U8, align_bytes=64)
-        for t in range(PACK - 1):
+        for t in range(PACK):
             nc.scalar.activation(note_planes[:, t, :], note_pool[t][:].indirect(note_list[:]), COPY)
-        nc.vector.tensor_copy(note_planes[:, PACK - 1, :], note_pool[PACK - 1][:].indirect(note_list[:]))
         interleave(nc.vector.tensor_copy, note_grouped[:], note_planes[:])
         nc.vector.quantize_mx(
             out=note_codes[:].bitcast(FP8X4), scales=note_scales[:], in_=note_grouped[:].rearrange("p j t -> p (j t)")
         )
 
-        vals_listed = tiles("vals_listed", [P, I], BF16)
-        val_codes = tiles("val_codes", [P, P], U32)
-        val_scales = tiles("val_scales", [P, P], U8)
-
-        def gather_vals(r):
-            if r < 2:
-                nc.scalar.activation(vals_listed[r][:], val_pool[r][:].indirect(token_list[:]), COPY)
-            else:
-                nc.vector.tensor_copy(vals_listed[r][:], val_pool[r][:].indirect(token_list[:]))
-
-        def prepare(r):
-            pairs = vals_listed[r][:].bitcast(F32)
-            turned = ps.tile([P, 2, P], F32, name="turned%d" % r, tag="turned%d" % (r % 2))
-            for u in range(2):
-                nc.tensor.transpose(turned[:, u, :], pairs[:, u : I // 2 : 2], identity[:])
-            tag = "val_pool%d" % (r + 1) if r in (1, 2) else "val_grouped%d" % r
-            grouped = sb.tile([P, P, PACK], BF16, name="val_grouped%d" % r, tag=tag, align_bytes=64)
-            copy = nc.scalar.copy if r == 0 else nc.vector.tensor_copy
-            copy(out=grouped[:].bitcast(F32), in_=turned[:].rearrange("p u e -> p e u"))
-            nc.vector.quantize_mx(
-                out=val_codes[r][:].bitcast(FP8X4),
-                scales=val_scales[r][:],
-                in_=grouped[:].rearrange("p e t -> p (e t)"),
-            )
-
         given_listed = tiles("given_listed", [P, J], F32)
         table_planes = sb.tile([P, PACK, J], F32, align_bytes=64)
+        table_grouped = sb.tile([P, J, PACK], BF16, align_bytes=64)
         table_codes = sb.tile([P, J], U32, align_bytes=64)
         table_scales = sb.tile([P, J], U8, align_bytes=64)
         halves = [slice(0, J // 2), slice(J // 2, J)]
@@ -174,66 +151,73 @@ def tile_attend_tab_timestable_put_pl_kernel(
                 op0=MULT,
                 op1=MULT,
             )
-
-        def quantise_table(h, tag):
-            grouped = sb.tile([P, J // 2, PACK], BF16, name="table_grouped%d" % h, tag=tag, align_bytes=64)
-            interleave(nc.vector.tensor_copy, grouped[:], table_planes[:, :, halves[h]])
+        for cols in halves:
+            interleave(nc.vector.tensor_copy, table_grouped[:, cols, :], table_planes[:, :, cols])
+        for cols in halves:
             nc.vector.quantize_mx(
-                out=table_codes[:, halves[h]].bitcast(FP8X4),
-                scales=table_scales[:, halves[h]],
-                in_=grouped[:].rearrange("p j t -> p (j t)"),
+                out=table_codes[:, cols].bitcast(FP8X4),
+                scales=table_scales[:, cols],
+                in_=table_grouped[:, cols, :].rearrange("p j t -> p (j t)"),
             )
 
-        def multiply(r, bank, cols):
+        vals_listed = tiles("vals_listed", [P, I], BF16)
+        val_codes = tiles("val_codes", [P, P], U32)
+        val_scales = tiles("val_scales", [P, P], U8)
+
+        def gather_vals(r):
+            if r < 2:
+                nc.scalar.activation(vals_listed[r][:], val_pool[r][:].indirect(token_list[:]), COPY)
+            else:
+                nc.vector.tensor_copy(vals_listed[r][:], val_pool[r][:].indirect(token_list[:]))
+
+        def turn_and_quantise(r, engine_copy, buffer):
+            pairs = vals_listed[r][:].bitcast(F32)
+            turned = ps.tile([P, 2, P], F32, name="turned%d" % r, tag="turned%d" % (r % 2))
+            for u in range(2):
+                nc.tensor.transpose(turned[:, u, :], pairs[:, u : I // 2 : 2], identity[:])
+            grouped = sb.tile([P, P, PACK], BF16, name="val_grouped%d" % r, tag=buffer, align_bytes=64)
+            engine_copy(out=grouped[:].bitcast(F32), in_=turned[:].rearrange("p u e -> p e u"))
+            nc.vector.quantize_mx(
+                out=val_codes[r][:].bitcast(FP8X4),
+                scales=val_scales[r][:],
+                in_=grouped[:].rearrange("p e t -> p (e t)"),
+            )
+
+        def multiply(r, bank_tag, engine_copy, buffer):
+            bank = ps.tile([P, J], F32, name="sums_bank%d" % r, tag=bank_tag)
             nc.tensor.matmul_mx(
                 out=bank[:],
                 lhsT=val_codes[r][:].bitcast(FP8X4),
                 lhsT_scale=val_scales[r][:],
-                rhs=table_codes[:, cols].bitcast(FP8X4),
-                rhs_scale=table_scales[:, cols],
+                rhs=table_codes[:].bitcast(FP8X4),
+                rhs_scale=table_scales[:],
                 start=True,
                 stop=True,
             )
+            sums = sb.tile([P, J], F32, name="sums%d" % r, tag=buffer, align_bytes=64)
+            engine_copy(out=sums[:], in_=bank[:])
+            return sums
 
-        def scatter_on_scalar(r, h, source):
-            nc.scalar.activation(placed[r][:].indirect(place_list[:, list_halves[h]]), source, COPY)
+        def scatter_on_scalar(r, sums):
+            for cols, entries in zip(halves, list_halves):
+                nc.scalar.activation(placed[r][:].indirect(place_list[:, entries]), sums[:, cols], COPY)
 
-        quantise_table(0, "table_grouped0")
         gather_vals(0)
-        prepare(0)
-        quantise_table(1, "val_grouped0")
+        turn_and_quantise(0, nc.scalar.copy, "val_grouped0")
         gather_vals(1)
-        for h in range(2):
-            sums = sb.tile([P, J // 2], F32, name="sums0_%d" % h, tag="val_pool1", align_bytes=64)
-            bank = ps.tile([P, J // 2], F32, name="half_sums%d" % h, tag="products%d" % h)
-            multiply(0, bank, halves[h])
-            nc.scalar.copy(out=sums[:], in_=bank[:])
-            scatter_on_scalar(0, h, sums[:])
+        scatter_on_scalar(0, multiply(0, "products0", nc.scalar.copy, "val_pool1"))
         gather_vals(2)
-        prepare(1)
-        bank = ps.tile([P, J], F32, name="bank1")
-        multiply(1, bank, slice(0, J))
-        sums = sb.tile([P, J], F32, name="sums1", align_bytes=64)
-        nc.scalar.copy(out=sums[:], in_=bank[:])
-        for h in range(2):
-            scatter_on_scalar(1, h, sums[:, halves[h]])
+        turn_and_quantise(1, nc.vector.tensor_copy, "val_pool2")
+        scatter_on_scalar(1, multiply(1, "sums_bank1", nc.scalar.copy, "sums1"))
         gather_vals(3)
-        prepare(2)
-        prepare(3)
-        bank = ps.tile([P, J], F32, name="bank2", tag="turned1")
-        multiply(2, bank, slice(0, J))
-        sums = sb.tile([P, J], F32, name="sums2", align_bytes=64)
-        nc.vector.tensor_copy(out=sums[:], in_=bank[:])
-        for h in range(2):
-            scatter_on_scalar(2, h, sums[:, halves[h]])
-        bank = ps.tile([P, J], F32, name="bank3")
-        multiply(3, bank, slice(0, J))
-        sums = sb.tile([P, J], F32, name="sums3", align_bytes=64)
-        nc.vector.tensor_copy(out=sums[:], in_=bank[:])
-        nc.vector.tensor_copy(placed[3][:].indirect(place_list[:]), sums[:])
+        turn_and_quantise(2, nc.vector.tensor_copy, "val_pool3")
+        turn_and_quantise(3, nc.vector.tensor_copy, "val_grouped3")
+        scatter_on_scalar(2, multiply(2, "turned1", nc.vector.tensor_copy, "sums2"))
+        last_sums = multiply(LAST, "sums_bank3", nc.vector.tensor_copy, "sums3")
+        nc.vector.tensor_copy(placed[LAST][:].indirect(place_list[:]), last_sums[:])
 
         y = sb.tile([P, PACK, M], F32, tag="val_grouped3", align_bytes=64)
-        nc.sync.dma_start(out=y[:, 2, :], in_=old_by_place[3])
+        nc.sync.dma_start(out=y[:, 2, :], in_=old_by_place[LAST])
         for r in range(2):
             nc.gpsimd.tensor_tensor(out=y[:, r, :], in0=old_rows[:, r, :], in1=placed[r][:], op=ADD)
             nc.sync.dma_start(out=out_by_place[:, r, :], in_=y[:, r, :])
@@ -242,26 +226,25 @@ def tile_attend_tab_timestable_put_pl_kernel(
         y_codes = sb.tile([P, M], U32, align_bytes=64)
         y_scales = sb.tile([P, M], U8, align_bytes=64)
         words_out = out_1[0].rearrange("p m t -> p (m t)").bitcast(I32)
-        quarter = M // 4
-        nc.vector.tensor_tensor(out=y[:, 3, :], in0=y[:, 2, :], in1=placed[3][:], op=ADD)
-        nc.sync.dma_start(out=out_by_place[:, 3, :], in_=y[:, 3, :])
-        for c in range(4):
-            cols = slice(c * quarter, (c + 1) * quarter)
+        quarters = [slice(c * M // 4, (c + 1) * M // 4) for c in range(4)]
+        nc.vector.tensor_tensor(out=y[:, LAST, :], in0=y[:, 2, :], in1=placed[LAST][:], op=ADD)
+        nc.sync.dma_start(out=out_by_place[:, LAST, :], in_=y[:, LAST, :])
+        for cols in quarters:
             nc.vector.tensor_tensor(out=y[:, 2, cols], in0=old_rows[:, 2, cols], in1=placed[2][:, cols], op=ADD)
         nc.sync.dma_start(out=out_by_place[:, 2, :], in_=y[:, 2, :])
-        split = 608
-        for lo, hi in ((0, 256), (256, 512), (512, split)):
-            interleave(nc.scalar.copy, y_grouped[:, lo:hi, :], y[:, :, lo:hi])
-        interleave(nc.vector.tensor_copy, y_grouped[:, split:M, :], y[:, :, split:M])
-        for c in (0, 3, 1, 2):
-            cols = slice(c * quarter, (c + 1) * quarter)
+
+        for cols in quarters[:2]:
+            interleave(nc.scalar.copy, y_grouped[:, cols, :], y[:, :, cols])
+        interleave(nc.vector.tensor_copy, y_grouped[:, M // 2 : M, :], y[:, :, M // 2 : M])
+        for c in (0, 2, 3, 1):
+            cols = quarters[c]
             nc.vector.quantize_mx(
                 out=y_codes[:, cols].bitcast(FP8X4),
                 scales=y_scales[:, cols],
                 in_=y_grouped[:, cols, :].rearrange("p m t -> p (m t)"),
             )
             nc.sync.dma_start(out=words_out[:, cols], in_=y_codes[:, cols].bitcast(I32))
-        for q in range(4):
+        for q in range(QUADRANTS):
             queue = nc.sync if q % 2 == 0 else nc.scalar
             queue.dma_start(
                 out=out_2[0, 4 * q : 4 * q + 4, :].bitcast(I32), in_=y_scales[32 * q : 32 * q + 4, :].bitcast(I32)

from contextlib import ExitStack

import concourse.mybir as mybir
from concourse.masks import make_identity

D, T, I, J, U, Z, E, M = 512, 2048, 512, 512, 1024, 1024, 512, 1024
FLOPS = 2 * D * I * J + 2 * I * E * J

F32 = mybir.dt.float32
BF16 = mybir.dt.bfloat16
I32 = mybir.dt.int32
U32 = mybir.dt.uint32
U16 = mybir.dt.uint16
U8 = mybir.dt.uint8
FP8X4 = mybir.dt.float8_e4m3fn_x4
FP4X4 = mybir.dt.float4_e2m1fn_x4
COPY = mybir.ActivationFunctionType.Copy
MULT = mybir.AluOpType.mult
ADD = mybir.AluOpType.add

P = 128
PACK = 4
QUADRANTS = 4
LIST_COLS = I // 16
LAST = PACK - 1


def interleave(engine_copy, grouped, planes):
    engine_copy(
        out=grouped.rearrange("p (c i) t -> p c t i", i=4),
        in_=planes.rearrange("p t (c i) -> p c t i", i=4),
    )


def tile_attend_tab_timestable_put_pl_kernel(
    tc, keys_words, keys_scales, notes, given, rowf, vals, old, offs, offs2, offs3, offs4, out_0, out_1, out_2
):
    nc = tc.nc
    with ExitStack() as ctx:
        sb = ctx.enter_context(tc.tile_pool(name="sb", bufs=1))
        ps = ctx.enter_context(tc.psum_pool(name="ps", bufs=1))

        def tiles(name, shape, dtype):
            return [sb.tile(shape, dtype, name="%s%d" % (name, t), align_bytes=64) for t in range(PACK)]

        token_list = sb.tile([P, LIST_COLS], U16)
        note_list = sb.tile([P, LIST_COLS], U16)
        given_list = sb.tile([P, LIST_COLS], U16)
        place_list = sb.tile([P, LIST_COLS], U16)
        key_word_pool = sb.tile([P, T], U16, align_bytes=64)
        key_scale_pool = sb.tile([P, T], U8, align_bytes=64)
        note_pool = tiles("note_pool", [P, U], F32)
        given_pool = tiles("given_pool", [P, Z], F32)
        val_pool = tiles("val_pool", [P, T], F32)
        placed = tiles("placed", [P, M], F32)
        old_rows = sb.tile([P, LAST, M], F32, align_bytes=64)
        row_factor = sb.tile([P, PACK], F32)
        identity = sb.tile([P, P], F32)

        notes_by_place = notes.rearrange("(p t) u -> t p u", t=PACK)
        given_by_place = given.rearrange("(p t) z -> t p z", t=PACK)
        vals_by_place = vals.rearrange("(p t) c -> t p c", t=PACK)
        old_by_place = old.rearrange("(p t) m -> t p m", t=PACK)
        out_by_place = out_0.rearrange("(p t) m -> p t m", t=PACK)

        make_identity(nc, identity[:])
        nc.vector.memset(key_scale_pool[:].bitcast(I32), 0)
        key_scale_rows = sb.tile([P, T // 4], I32, align_bytes=64)

        def load_key_scales(q):
            nc.sync.dma_start(
                out=key_scale_rows[32 * q : 32 * q + 4, :],
                in_=keys_scales[0, 4 * q : 4 * q + 4, :].bitcast(I32),
            )

        nc.sync.dma_start(note_list[:], offs2)
        nc.sync.dma_start(token_list[:], offs)
        nc.sync.dma_start(out=note_pool[0][:], in_=notes_by_place[0])
        nc.sync.dma_start(out=key_word_pool[:].bitcast(I32), in_=keys_words[0].bitcast(I32))
        nc.sync.dma_start(out=note_pool[1][:], in_=notes_by_place[1])
        load_key_scales(0)
        load_key_scales(1)
        nc.sync.dma_start(out=note_pool[2][:], in_=notes_by_place[2])
        load_key_scales(2)
        load_key_scales(3)
        nc.sync.dma_start(out=note_pool[3][:], in_=notes_by_place[3])
        nc.sync.dma_start(out=given_pool[0][:], in_=given_by_place[0])
        nc.sync.dma_start(given_list[:], offs3)
        nc.sync.dma_start(out=given_pool[1][:], in_=given_by_place[1])
        nc.sync.dma_start(out=given_pool[2][:], in_=given_by_place[2])
        nc.sync.dma_start(out=row_factor[:], in_=rowf.rearrange("(p t) o -> p (t o)", t=PACK))
        nc.sync.dma_start(out=given_pool[3][:], in_=given_by_place[3])
        nc.sync.dma_start(out=val_pool[0][:], in_=vals_by_place[0])
        nc.sync.dma_start(place_list[:], offs4)
        for r in range(1, PACK):
            nc.sync.dma_start(out=val_pool[r][:], in_=vals_by_place[r])
        for r in range(LAST):
            nc.sync.dma_start(out=old_rows[:, r, :], in_=old_by_place[r])

        for r in range(PACK):
            engine = nc.vector if r < 2 else nc.gpsimd
            engine.memset(placed[r][:], 0.0)

        key_words_listed = sb.tile([P, I], U16, align_bytes=64)
        key_words = sb.tile([P, PACK, P], U16, align_bytes=64)
        key_scales = sb.tile([P, PACK, P], U8, align_bytes=64)
        nc.vector.tensor_copy(key_words_listed[:], key_word_pool[:].indirect(token_list[:]))
        nc.vector.tensor_copy(out=key_words[:], in_=key_words_listed[:].rearrange("p (s t) -> p t s", t=PACK))
        for q in range(QUADRANTS):
            rows = slice(32 * q, 32 * q + 4)
            nc.vector.tensor_copy(out=key_scale_pool[rows, :].bitcast(I32), in_=key_scale_rows[rows, :])
        key_scales_listed = sb.tile([P, I], U8, align_bytes=64)
        nc.vector.tensor_copy(key_scales_listed[:], key_scale_pool[:].indirect(token_list[:]))
        nc.vector.tensor_copy(out=key_scales[:], in_=key_scales_listed[:].rearrange("p (s t) -> p t s", t=PACK))

        note_planes = sb.tile([P, PACK, J], F32, align_bytes=64)
        note_grouped = sb.tile([P, J, PACK], BF16, align_bytes=64)
        note_codes = sb.tile([P, J], U32, align_bytes=64)
        note_scales = sb.tile([P, J], U8, align_bytes=64)
        for t in range(PACK):
            nc.scalar.activation(note_planes[:, t, :], note_pool[t][:].indirect(note_list[:]), COPY)
        interleave(nc.vector.tensor_copy, note_grouped[:], note_planes[:])
        nc.vector.quantize_mx(
            out=note_codes[:].bitcast(FP8X4), scales=note_scales[:], in_=note_grouped[:].rearrange("p j t -> p (j t)")
        )

        given_listed = tiles("given_listed", [P, J], F32)
        table_planes = sb.tile([P, PACK, J], F32, align_bytes=64)
        table_grouped = sb.tile([P, J, PACK], BF16, align_bytes=64)
        table_codes = sb.tile([P, J], U32, align_bytes=64)
        table_scales = sb.tile([P, J], U8, align_bytes=64)
        halves = [slice(0, J // 2), slice(J // 2, J)]
        list_halves = [slice(0, LIST_COLS // 2), slice(LIST_COLS // 2, LIST_COLS)]
        for t in range(PACK):
            products = ps.tile([P, J], F32, name="products%d" % t)
            nc.tensor.matmul_mx(
                out=products[:],
                lhsT=key_words[:, t, :].bitcast(FP4X4),
                lhsT_scale=key_scales[:, t, :],
                rhs=note_codes[:].bitcast(FP8X4),
                rhs_scale=note_scales[:],
                start=True,
                stop=True,
            )
            nc.scalar.activation(given_listed[t][:], given_pool[t][:].indirect(given_list[:]), COPY)
            nc.vector.scalar_tensor_tensor(
                out=table_planes[:, t, :],
                in0=products[:],
                scalar=row_factor[:, t : t + 1],
                in1=given_listed[t][:],
                op0=MULT,
                op1=MULT,
            )
        for cols in halves:
            interleave(nc.vector.tensor_copy, table_grouped[:, cols, :], table_planes[:, :, cols])
        for cols in halves:
            nc.vector.quantize_mx(
                out=table_codes[:, cols].bitcast(FP8X4),
                scales=table_scales[:, cols],
                in_=table_grouped[:, cols, :].rearrange("p j t -> p (j t)"),
            )

        vals_listed = tiles("vals_listed", [P, I], BF16)
        val_codes = tiles("val_codes", [P, P], U32)
        val_scales = tiles("val_scales", [P, P], U8)

        def gather_vals(r):
            if r < 2:
                nc.scalar.activation(vals_listed[r][:], val_pool[r][:].indirect(token_list[:]), COPY)
            else:
                nc.vector.tensor_copy(vals_listed[r][:], val_pool[r][:].indirect(token_list[:]))

        def turn_and_quantise(r, engine_copy, buffer):
            pairs = vals_listed[r][:].bitcast(F32)
            turned = ps.tile([P, 2, P], F32, name="turned%d" % r, tag="turned%d" % (r % 2))
            for u in range(2):
                nc.tensor.transpose(turned[:, u, :], pairs[:, u : I // 2 : 2], identity[:])
            grouped = sb.tile([P, P, PACK], BF16, name="val_grouped%d" % r, tag=buffer, align_bytes=64)
            engine_copy(out=grouped[:].bitcast(F32), in_=turned[:].rearrange("p u e -> p e u"))
            nc.vector.quantize_mx(
                out=val_codes[r][:].bitcast(FP8X4),
                scales=val_scales[r][:],
                in_=grouped[:].rearrange("p e t -> p (e t)"),
            )

        def multiply(r, bank_tag, engine_copy, buffer):
            bank = ps.tile([P, J], F32, name="sums_bank%d" % r, tag=bank_tag)
            nc.tensor.matmul_mx(
                out=bank[:],
                lhsT=val_codes[r][:].bitcast(FP8X4),
                lhsT_scale=val_scales[r][:],
                rhs=table_codes[:].bitcast(FP8X4),
                rhs_scale=table_scales[:],
                start=True,
                stop=True,
            )
            sums = sb.tile([P, J], F32, name="sums%d" % r, tag=buffer, align_bytes=64)
            engine_copy(out=sums[:], in_=bank[:])
            return sums

        def scatter_on_scalar(r, sums):
            for cols, entries in zip(halves, list_halves):
                nc.scalar.activation(placed[r][:].indirect(place_list[:, entries]), sums[:, cols], COPY)

        gather_vals(0)
        turn_and_quantise(0, nc.scalar.copy, "val_grouped0")
        gather_vals(1)
        scatter_on_scalar(0, multiply(0, "products0", nc.scalar.copy, "val_pool1"))
        gather_vals(2)
        turn_and_quantise(1, nc.vector.tensor_copy, "val_pool2")
        scatter_on_scalar(1, multiply(1, "sums_bank1", nc.scalar.copy, "sums1"))
        gather_vals(3)
        turn_and_quantise(2, nc.vector.tensor_copy, "val_pool3")
        turn_and_quantise(3, nc.vector.tensor_copy, "val_grouped3")
        scatter_on_scalar(2, multiply(2, "turned1", nc.vector.tensor_copy, "sums2"))
        last_sums = multiply(LAST, "sums_bank3", nc.vector.tensor_copy, "sums3")
        nc.vector.tensor_copy(placed[LAST][:].indirect(place_list[:]), last_sums[:])

        y = sb.tile([P, PACK, M], F32, tag="val_grouped3", align_bytes=64)
        nc.sync.dma_start(out=y[:, 2, :], in_=old_by_place[LAST])
        for r in range(2):
            nc.gpsimd.tensor_tensor(out=y[:, r, :], in0=old_rows[:, r, :], in1=placed[r][:], op=ADD)
            nc.sync.dma_start(out=out_by_place[:, r, :], in_=y[:, r, :])

        y_grouped = sb.tile([P, M, PACK], BF16, align_bytes=64)
        y_codes = sb.tile([P, M], U32, align_bytes=64)
        y_scales = sb.tile([P, M], U8, align_bytes=64)
        words_out = out_1[0].rearrange("p m t -> p (m t)").bitcast(I32)
        quarters = [slice(c * M // 4, (c + 1) * M // 4) for c in range(4)]
        nc.vector.tensor_tensor(out=y[:, LAST, :], in0=y[:, 2, :], in1=placed[LAST][:], op=ADD)
        nc.sync.dma_start(out=out_by_place[:, LAST, :], in_=y[:, LAST, :])
        for cols in quarters:
            nc.vector.tensor_tensor(out=y[:, 2, cols], in0=old_rows[:, 2, cols], in1=placed[2][:, cols], op=ADD)
        nc.sync.dma_start(out=out_by_place[:, 2, :], in_=y[:, 2, :])

        for cols in quarters[:2]:
            interleave(nc.scalar.copy, y_grouped[:, cols, :], y[:, :, cols])
        interleave(nc.vector.tensor_copy, y_grouped[:, M // 2 : M, :], y[:, :, M // 2 : M])
        for c in (0, 2, 3, 1):
            cols = quarters[c]
            nc.vector.quantize_mx(
                out=y_codes[:, cols].bitcast(FP8X4),
                scales=y_scales[:, cols],
                in_=y_grouped[:, cols, :].rearrange("p m t -> p (m t)"),
            )
            nc.sync.dma_start(out=words_out[:, cols], in_=y_codes[:, cols].bitcast(I32))
        for q in range(QUADRANTS):
            queue = nc.sync if q % 2 == 0 else nc.scalar
            queue.dma_start(
                out=out_2[0, 4 * q : 4 * q + 4, :].bitcast(I32), in_=y_scales[32 * q : 32 * q + 4, :].bitcast(I32)
            )
